import numpy as np
import ml_dtypes


def mxq(x, axis, fmt="e4m3"):
    dtype, down = {"e4m3": (ml_dtypes.float8_e4m3fn, 7), "e5m2": (ml_dtypes.float8_e5m2, 14)}[fmt]
    v = np.moveaxis(np.asarray(x, np.float32).astype(ml_dtypes.bfloat16).astype(np.float64), axis, -1)
    blocks = v.reshape(v.shape[:-1] + (-1, 32))
    amax = np.abs(blocks).max(-1, keepdims=True)
    byte = np.maximum(np.where(amax > 0, np.frexp(amax)[1] - 1 + 127, 0) - down, 1)
    scale = np.exp2(byte - 127.0)
    codes = (blocks / scale).astype(np.float32).astype(dtype).astype(np.float64)
    return np.moveaxis((codes * scale).reshape(v.shape), -1, axis)


WIDE = False


def mx_kscale(k):
    if not WIDE:
        return np.ones(k)
    levels = np.array([30, -30])
    if k % 512:
        return np.exp2(np.random.permutation(np.resize(levels, k // 32))).repeat(32)
    a = np.empty((k // 512, 16))
    for p in range(k // 512):
        a[p, :8] = np.random.permutation(np.resize(levels, 8))
        for g in range(8):
            far = levels[np.abs(levels - a[p, g]) >= 10]
            a[p, g + 8] = far[np.random.randint(len(far))]
    return np.exp2(a.ravel()).repeat(32)


def f64(x):
    return np.asarray(x).astype(np.float64)


def striped(idx):
    return np.tile(np.asarray(idx).reshape(-1, 16).T, (8, 1)).astype(np.uint16)


def unstriped(offs):
    return offs[:16].T.reshape(-1).astype(np.int64)


E2M1 = np.array([0.0, 0.5, 1.0, 1.5, 2.0, 3.0, 4.0, 6.0, -0.0, -0.5, -1.0, -1.5, -2.0, -3.0, -4.0, -6.0])


def pack_weight(w, fmt):
    k, n = w.shape
    w = f64(np.asarray(w, np.float32).astype(ml_dtypes.bfloat16)).reshape(k // 32, 32, n)
    amax = np.abs(w).max(1)
    if fmt in ("e4m3", "e5m2"):
        byte = np.frexp(amax)[1] - 1 + 127 - (7 if fmt == "e4m3" else 14)
    else:
        mant, ex = np.frexp(amax / 6.0)
        byte = np.where(mant > 0.5, ex, ex - 1) + 127
    byte = np.clip(np.where(amax > 0, byte, 1), 1, 254)
    scaled = (w * np.exp2(127.0 - byte)[:, None, :]).reshape(k, n).astype(np.float32)
    by_word = np.ascontiguousarray(scaled.reshape(k // 512, 128, 4, n).transpose(0, 1, 3, 2))
    if fmt in ("e4m3", "e5m2"):
        words = by_word.astype(ml_dtypes.float8_e4m3fn if fmt == "e4m3" else ml_dtypes.float8_e5m2).view(np.uint8)
    else:
        c = by_word.astype(ml_dtypes.float4_e2m1fn).view(np.uint8) & 0xF
        words = (c[..., 0::2] | (c[..., 1::2] << 4)).reshape(k // 512, 128, 2 * n)
    return np.ascontiguousarray(words), np.ascontiguousarray(byte.astype(np.uint8).reshape(k // 512, 16, n))


def unpack_weight(words, scales, fmt):
    g, _, n = scales.shape
    words = np.ascontiguousarray(words).reshape(g, 128, n, -1)
    if fmt in ("e4m3", "e5m2"):
        vals = words.view(ml_dtypes.float8_e4m3fn if fmt == "e4m3" else ml_dtypes.float8_e5m2).astype(np.float64)
    else:
        nib = np.empty((g, 128, n, 4), np.uint8)
        nib[..., 0::2] = words & 0xF
        nib[..., 1::2] = words >> 4
        vals = E2M1[nib]
    vals = vals * np.repeat(np.exp2(scales.astype(np.float64) - 127.0), 8, axis=1)[..., None]
    return vals.transpose(0, 1, 3, 2).reshape(g * 512, n)


K, T, I, J, N, Z, S = 512, 1024, 512, 256, 256, 1024, 1024


def setup_inputs():
    n = np.random.standard_normal
    idx = np.random.permutation(T)[:I]
    idx2 = np.random.permutation(Z)[:J]
    idx3 = np.random.permutation(Z)[:J]
    idx4 = np.random.permutation(S)[:N]
    fk = mx_kscale(K)
    fi = mx_kscale(I)
    ti = np.ones(T)
    ti[idx] = fi
    xkp = pack_weight(n((K, T)) * 0.3 * fk[:, None] * ti, "e2m1")
    xqp = pack_weight(n((K, Z)) * 0.3 / fk[:, None], "e5m2")
    vsp = pack_weight(n((I, S)) / fi[:, None], "e2m1")
    return {
        "xk_words": xkp[0],
        "xk_scales": xkp[1],
        "xq_words": xqp[0],
        "xq_scales": xqp[1],
        "vs_words": vsp[0],
        "vs_scales": vsp[1],
        "offs": striped(idx),
        "offs2": striped(idx2),
        "offs3": striped(idx3),
        "offs4": striped(idx4),
    }


def reference(xk_words, xk_scales, xq_words, xq_scales, vs_words, vs_scales, offs, offs2, offs3, offs4):
    idx = unstriped(offs)
    idx2 = unstriped(offs2)
    idx3 = unstriped(offs3)
    idx4 = unstriped(offs4)
    xku = unpack_weight(xk_words, xk_scales, "e2m1")
    xqu = unpack_weight(xq_words, xq_scales, "e5m2")
    vsu = unpack_weight(vs_words, vs_scales, "e2m1")
    xkidxg = xku[:, idx]
    xqidx2g = xqu[:, idx2]
    s1 = xkidxg.T @ xqidx2g
    xqidx3g = xqu[:, idx3]
    s2 = xkidxg.T @ xqidx3g
    hid = np.abs(s1 - s2)
    vsidx4g = vsu[:, idx4]
    hidq = mxq(hid, 0, "e5m2")
    y = vsidx4g.T @ hidq
    return y

@@ -1,0 +1,148 @@
+from contextlib import ExitStack
+
+import concourse.mybir as mybir
+
+F32 = mybir.dt.float32
+BF16 = mybir.dt.bfloat16
+I32 = mybir.dt.int32
+U32 = mybir.dt.uint32
+U16 = mybir.dt.uint16
+U8 = mybir.dt.uint8
+FP4X4 = mybir.dt.float4_e2m1fn_x4
+FP8X4 = mybir.dt.float8_e5m2_x4
+ACT = mybir.ActivationFunctionType
+ALU = mybir.AluOpType
+
+P = 128
+PACK = 4
+COLS = 1024
+I, J, N = 512, 256, 256
+HALF = 128
+LIST_ROWS = 16
+LINE = 8
+
+FLOPS = 2 * 512 * I * J * 2 + 2 * I * N * J
+
+
+def tile_list_contest_twice_direct_plain_kernel(
+    tc, xk_words, xk_scales, xq_words, xq_scales, vs_words, vs_scales, offs, offs2, offs3, offs4, out
+):
+    nc = tc.nc
+    with ExitStack() as ctx:
+        lists = ctx.enter_context(tc.tile_pool(name="lists", bufs=1))
+        sb = ctx.enter_context(tc.tile_pool(name="sb", bufs=1))
+        ps = ctx.enter_context(tc.psum_pool(name="ps", bufs=1))
+
+        def load_list(name, src):
+            tile = lists.tile(list(src.shape), U16, name=name)
+            nc.sync.dma_start(tile[:], src)
+            return tile
+
+        def load_words(name, src, dtype):
+            tile = sb.tile([P, COLS], dtype, name=name, align_bytes=64)
+            nc.sync.dma_start(tile[:].bitcast(I32), src.bitcast(I32))
+            return tile
+
+        def load_scales(name, src, queue):
+            tile = sb.tile([P, COLS], U8, name=name, align_bytes=64)
+            nc.vector.memset(tile[:].bitcast(I32), 0)
+            for quad in range(4):
+                queue.dma_start(
+                    tile[32 * quad : 32 * quad + 4, :].bitcast(I32),
+                    src[0, 4 * quad : 4 * quad + 4, :].bitcast(I32),
+                )
+            return tile
+
+        def gather(name, window, offsets, width, dtype):
+            tile = sb.tile([P, width], dtype, name=name, align_bytes=64)
+            nc.vector.tensor_copy(tile[:], window[:].indirect(offsets))
+            return tile
+
+        k_list = load_list("k_list", offs)
+        k_words = load_words("k_words", xk_words[0], U16)
+        k_scales = load_scales("k_scales", xk_scales, nc.scalar)
+        q3_list = load_list("q3_list", offs3)
+        q_words = load_words("q_words", xq_words[0].rearrange("p c r -> p (c r)"), U32)
+        q_scales = load_scales("q_scales", xq_scales, nc.scalar)
+        q2_list = load_list("q2_list", offs2)
+        v_list = load_list("v_list", offs4)
+        v_words = load_words("v_words", vs_words[0], U16)
+        v_scales = load_scales("v_scales", vs_scales, nc.sync)
+
+        k_picked = gather("k_picked", k_words, k_list[:], I, U16)
+        k_dealt_scales = sb.tile([P, I], U8, name="k_dealt_scales", align_bytes=64)
+        nc.vector.tensor_copy(
+            k_dealt_scales[:].rearrange("p (t m) -> p m t", t=PACK), k_scales[:].indirect(k_list[:])
+        )
+        k_dealt = sb.tile([P, I], U16, name="k_dealt", align_bytes=64)
+        nc.vector.tensor_copy(
+            k_dealt[:].rearrange("p (t a b) -> p a t b", t=PACK, b=LINE),
+            k_picked[:].rearrange("p (a b t) -> p a t b", t=PACK, b=LINE),
+        )
+
+        def scores(name, q_list, half):
+            cut = q_list[:, half * HALF // LIST_ROWS : (half + 1) * HALF // LIST_ROWS]
+            words = gather(name + "_words", q_words, cut, HALF, U32)
+            scales = gather(name + "_scales", q_scales, cut, HALF, U8)
+            bank = ps.tile([P, PACK, HALF], F32, name=name + "_bank")
+            for t in range(PACK):
+                rows = slice(t * P, (t + 1) * P)
+                nc.tensor.matmul_mx(
+                    out=bank[:, t, :],
+                    lhsT=k_dealt[:, rows].bitcast(FP4X4),
+                    lhsT_scale=k_dealt_scales[:, rows],
+                    rhs=words[:].bitcast(FP8X4),
+                    rhs_scale=scales[:],
+                    start=True,
+                    stop=True,
+                )
+            return bank[:].rearrange("p t j -> p j t")
+
+        s1, s2 = [], []
+        for half in range(2):
+            s2_bank = scores("s2_%d" % half, q3_list, half)
+            s1.append(scores("s1_%d" % half, q2_list, half))
+            s2_sb = sb.tile([P, HALF, PACK], F32, name="s2_sb_%d" % half)
+            nc.scalar.activation(s2_sb[:], s2_bank, ACT.Copy)
+            s2.append(s2_sb)
+
+        def magnitude(half):
+            diff = sb.tile([P, HALF, PACK], F32, name="diff_%d" % half)
+            nc.vector.tensor_tensor(diff[:], s1[half], s2[half][:], ALU.subtract)
+            hid = sb.tile([P, HALF * PACK], BF16, name="hid_%d" % half, align_bytes=64)
+            nc.scalar.activation(hid[:], diff[:].rearrange("p j t -> p (j t)"), ACT.Abs)
+            return hid
+
+        hid0 = magnitude(0)
+        v_picked = gather("v_picked", v_words, v_list[:], N, U16)
+        hid1 = magnitude(1)
+        v_picked_scales = gather("v_picked_scales", v_scales, v_list[:], N, U8)
+
+        quantised = []
+        for half, hid in enumerate((hid0, hid1)):
+            codes = sb.tile([P, HALF], U32, name="codes_%d" % half, align_bytes=64)
+            scales = sb.tile([P, HALF], U8, name="scales_%d" % half, align_bytes=64)
+            nc.vector.quantize_mx(out=codes[:].bitcast(FP8X4), scales=scales[:], in_=hid[:])
+            quantised.append((codes, scales))
+
+        for half, (codes, scales) in enumerate(quantised):
+            for part in range(2):
+                rows = slice(part * P, (part + 1) * P)
+                bank = ps.tile([P, HALF], F32, name="y_%d_%d" % (half, part))
+                nc.tensor.matmul_mx(
+                    out=bank[:],
+                    lhsT=v_picked[:, rows].bitcast(FP4X4),
+                    lhsT_scale=v_picked_scales[:, rows],
+                    rhs=codes[:].bitcast(FP8X4),
+                    rhs_scale=scales[:],
+                    start=True,
+                    stop=True,
+                )
+                result = sb.tile([P, HALF], F32, name="result_%d_%d" % (half, part))
+                dest = out[rows, half * HALF : (half + 1) * HALF]
+                if part == 0:
+                    nc.vector.tensor_copy(result[:], bank[:])
+                    nc.sync.dma_start(dest, result[:])
+                else:
+                    nc.scalar.copy(result[:], bank[:])
+                    nc.scalar.dma_start(dest, result[:])

@@ -60,10 +60,10 @@ def tile_list_contest_twice_direct_plain_kernel(
 
         k_list = load_list("k_list", offs)
         k_words = load_words("k_words", xk_words[0], U16)
-        k_scales = load_scales("k_scales", xk_scales, nc.scalar)
+        k_scales = load_scales("k_scales", xk_scales, nc.sync)
         q3_list = load_list("q3_list", offs3)
         q_words = load_words("q_words", xq_words[0].rearrange("p c r -> p (c r)"), U32)
-        q_scales = load_scales("q_scales", xq_scales, nc.scalar)
+        q_scales = load_scales("q_scales", xq_scales, nc.sync)
         q2_list = load_list("q2_list", offs2)
         v_list = load_list("v_list", offs4)
         v_words = load_words("v_words", vs_words[0], U16)

@@ -58,26 +58,29 @@ def tile_list_contest_twice_direct_plain_kernel(
             nc.vector.tensor_copy(tile[:], window[:].indirect(offsets))
             return tile
 
-        k_list = load_list("k_list", offs)
         k_words = load_words("k_words", xk_words[0], U16)
+        k_list = load_list("k_list", offs)
         k_scales = load_scales("k_scales", xk_scales, nc.sync)
-        q3_list = load_list("q3_list", offs3)
         q_words = load_words("q_words", xq_words[0].rearrange("p c r -> p (c r)"), U32)
         q_scales = load_scales("q_scales", xq_scales, nc.sync)
+        q3_list = load_list("q3_list", offs3)
         q2_list = load_list("q2_list", offs2)
         v_list = load_list("v_list", offs4)
         v_words = load_words("v_words", vs_words[0], U16)
         v_scales = load_scales("v_scales", vs_scales, nc.sync)
 
-        k_picked = gather("k_picked", k_words, k_list[:], I, U16)
+        k_picked = [
+            gather("k_picked_%d" % c, k_words, k_list[:, c * 16 : (c + 1) * 16], I // 2, U16) for c in range(2)
+        ]
+        k_dealt = sb.tile([P, PACK, P], U16, name="k_dealt", align_bytes=64)
+        for c in range(2):
+            nc.vector.tensor_copy(
+                k_dealt[:, :, c * 64 : (c + 1) * 64].rearrange("p t (a b) -> p a t b", b=LINE),
+                k_picked[c][:].rearrange("p (a b t) -> p a t b", t=PACK, b=LINE),
+            )
         k_dealt_scales = sb.tile([P, I], U8, name="k_dealt_scales", align_bytes=64)
         nc.vector.tensor_copy(
             k_dealt_scales[:].rearrange("p (t m) -> p m t", t=PACK), k_scales[:].indirect(k_list[:])
-        )
-        k_dealt = sb.tile([P, I], U16, name="k_dealt", align_bytes=64)
-        nc.vector.tensor_copy(
-            k_dealt[:].rearrange("p (t a b) -> p a t b", t=PACK, b=LINE),
-            k_picked[:].rearrange("p (a b t) -> p a t b", t=PACK, b=LINE),
         )
 
         def scores(name, q_list, half):
@@ -89,7 +92,7 @@ def tile_list_contest_twice_direct_plain_kernel(
                 rows = slice(t * P, (t + 1) * P)
                 nc.tensor.matmul_mx(
                     out=bank[:, t, :],
-                    lhsT=k_dealt[:, rows].bitcast(FP4X4),
+                    lhsT=k_dealt[:, t, :].bitcast(FP4X4),
                     lhsT_scale=k_dealt_scales[:, rows],
                     rhs=words[:].bitcast(FP8X4),
                     rhs_scale=scales[:],
@@ -98,19 +101,21 @@ def tile_list_contest_twice_direct_plain_kernel(
                 )
             return bank[:].rearrange("p t j -> p j t")
 
-        s1, s2 = [], []
+        s2 = []
         for half in range(2):
             s2_bank = scores("s2_%d" % half, q3_list, half)
-            s1.append(scores("s1_%d" % half, q2_list, half))
             s2_sb = sb.tile([P, HALF, PACK], F32, name="s2_sb_%d" % half)
             nc.scalar.activation(s2_sb[:], s2_bank, ACT.Copy)
             s2.append(s2_sb)
+        s1 = [scores("s1_%d" % half, q2_list, half) for half in range(2)]
 
         def magnitude(half):
-            diff = sb.tile([P, HALF, PACK], F32, name="diff_%d" % half)
-            nc.vector.tensor_tensor(diff[:], s1[half], s2[half][:], ALU.subtract)
-            hid = sb.tile([P, HALF * PACK], BF16, name="hid_%d" % half, align_bytes=64)
-            nc.scalar.activation(hid[:], diff[:].rearrange("p j t -> p (j t)"), ACT.Abs)
+            hid = sb.tile([P, HALF, PACK], BF16, name="hid_%d" % half, align_bytes=64)
+            for c in range(2):
+                cols = slice(c * HALF // 2, (c + 1) * HALF // 2)
+                diff = sb.tile([P, HALF // 2, PACK], F32, name="diff_%d_%d" % (half, c))
+                nc.vector.tensor_tensor(diff[:], s1[half][:, cols, :], s2[half][:, cols, :], ALU.subtract)
+                nc.scalar.activation(hid[:, cols, :], diff[:], ACT.Abs)
             return hid
 
         hid0 = magnitude(0)
@@ -122,7 +127,7 @@ def tile_list_contest_twice_direct_plain_kernel(
         for half, hid in enumerate((hid0, hid1)):
             codes = sb.tile([P, HALF], U32, name="codes_%d" % half, align_bytes=64)
             scales = sb.tile([P, HALF], U8, name="scales_%d" % half, align_bytes=64)
-            nc.vector.quantize_mx(out=codes[:].bitcast(FP8X4), scales=scales[:], in_=hid[:])
+            nc.vector.quantize_mx(out=codes[:].bitcast(FP8X4), scales=scales[:], in_=hid[:].rearrange("p j t -> p (j t)"))
             quantised.append((codes, scales))
 
         for half, (codes, scales) in enumerate(quantised):

from contextlib import ExitStack

import concourse.mybir as mybir

F32 = mybir.dt.float32
BF16 = mybir.dt.bfloat16
I32 = mybir.dt.int32
U32 = mybir.dt.uint32
U16 = mybir.dt.uint16
U8 = mybir.dt.uint8
FP4X4 = mybir.dt.float4_e2m1fn_x4
FP8X4 = mybir.dt.float8_e5m2_x4
ACT = mybir.ActivationFunctionType
ALU = mybir.AluOpType

P = 128
PACK = 4
COLS = 1024
I, J, N = 512, 256, 256
HALF = 128
LIST_ROWS = 16
LINE = 8

FLOPS = 2 * 512 * I * J * 2 + 2 * I * N * J


def tile_list_contest_twice_direct_plain_kernel(
    tc, xk_words, xk_scales, xq_words, xq_scales, vs_words, vs_scales, offs, offs2, offs3, offs4, out
):
    nc = tc.nc
    with ExitStack() as ctx:
        lists = ctx.enter_context(tc.tile_pool(name="lists", bufs=1))
        sb = ctx.enter_context(tc.tile_pool(name="sb", bufs=1))
        ps = ctx.enter_context(tc.psum_pool(name="ps", bufs=1))

        def load_list(name, src):
            tile = lists.tile(list(src.shape), U16, name=name)
            nc.sync.dma_start(tile[:], src)
            return tile

        def load_words(name, src, dtype):
            tile = sb.tile([P, COLS], dtype, name=name, align_bytes=64)
            nc.sync.dma_start(tile[:].bitcast(I32), src.bitcast(I32))
            return tile

        def load_scales(name, src, queue):
            tile = sb.tile([P, COLS], U8, name=name, align_bytes=64)
            nc.vector.memset(tile[:].bitcast(I32), 0)
            for quad in range(4):
                queue.dma_start(
                    tile[32 * quad : 32 * quad + 4, :].bitcast(I32),
                    src[0, 4 * quad : 4 * quad + 4, :].bitcast(I32),
                )
            return tile

        def gather(name, window, offsets, width, dtype):
            tile = sb.tile([P, width], dtype, name=name, align_bytes=64)
            nc.vector.tensor_copy(tile[:], window[:].indirect(offsets))
            return tile

        k_words = load_words("k_words", xk_words[0], U16)
        k_list = load_list("k_list", offs)
        k_scales = load_scales("k_scales", xk_scales, nc.sync)
        q_words = load_words("q_words", xq_words[0].rearrange("p c r -> p (c r)"), U32)
        q_scales = load_scales("q_scales", xq_scales, nc.sync)
        q3_list = load_list("q3_list", offs3)
        q2_list = load_list("q2_list", offs2)
        v_list = load_list("v_list", offs4)
        v_words = load_words("v_words", vs_words[0], U16)
        v_scales = load_scales("v_scales", vs_scales, nc.sync)

        k_picked = [
            gather("k_picked_%d" % c, k_words, k_list[:, c * 16 : (c + 1) * 16], I // 2, U16) for c in range(2)
        ]
        k_dealt = sb.tile([P, PACK, P], U16, name="k_dealt", align_bytes=64)
        for c in range(2):
            nc.vector.tensor_copy(
                k_dealt[:, :, c * 64 : (c + 1) * 64].rearrange("p t (a b) -> p a t b", b=LINE),
                k_picked[c][:].rearrange("p (a b t) -> p a t b", t=PACK, b=LINE),
            )
        k_dealt_scales = sb.tile([P, I], U8, name="k_dealt_scales", align_bytes=64)
        nc.vector.tensor_copy(
            k_dealt_scales[:].rearrange("p (t m) -> p m t", t=PACK), k_scales[:].indirect(k_list[:])
        )

        def scores(name, q_list, half):
            cut = q_list[:, half * HALF // LIST_ROWS : (half + 1) * HALF // LIST_ROWS]
            words = gather(name + "_words", q_words, cut, HALF, U32)
            scales = gather(name + "_scales", q_scales, cut, HALF, U8)
            bank = ps.tile([P, PACK, HALF], F32, name=name + "_bank")
            for t in range(PACK):
                rows = slice(t * P, (t + 1) * P)
                nc.tensor.matmul_mx(
                    out=bank[:, t, :],
                    lhsT=k_dealt[:, t, :].bitcast(FP4X4),
                    lhsT_scale=k_dealt_scales[:, rows],
                    rhs=words[:].bitcast(FP8X4),
                    rhs_scale=scales[:],
                    start=True,
                    stop=True,
                )
            return bank[:].rearrange("p t j -> p j t")

        s2 = []
        for half in range(2):
            s2_bank = scores("s2_%d" % half, q3_list, half)
            s2_sb = sb.tile([P, HALF, PACK], F32, name="s2_sb_%d" % half)
            nc.scalar.activation(s2_sb[:], s2_bank, ACT.Copy)
            s2.append(s2_sb)
        s1 = [scores("s1_%d" % half, q2_list, half) for half in range(2)]

        def magnitude(half):
            hid = sb.tile([P, HALF, PACK], BF16, name="hid_%d" % half, align_bytes=64)
            for c in range(2):
                cols = slice(c * HALF // 2, (c + 1) * HALF // 2)
                diff = sb.tile([P, HALF // 2, PACK], F32, name="diff_%d_%d" % (half, c))
                nc.vector.tensor_tensor(diff[:], s1[half][:, cols, :], s2[half][:, cols, :], ALU.subtract)
                nc.scalar.activation(hid[:, cols, :], diff[:], ACT.Abs)
            return hid

        hid0 = magnitude(0)
        v_picked = gather("v_picked", v_words, v_list[:], N, U16)
        hid1 = magnitude(1)
        v_picked_scales = gather("v_picked_scales", v_scales, v_list[:], N, U8)

        quantised = []
        for half, hid in enumerate((hid0, hid1)):
            codes = sb.tile([P, HALF], U32, name="codes_%d" % half, align_bytes=64)
            scales = sb.tile([P, HALF], U8, name="scales_%d" % half, align_bytes=64)
            nc.vector.quantize_mx(out=codes[:].bitcast(FP8X4), scales=scales[:], in_=hid[:].rearrange("p j t -> p (j t)"))
            quantised.append((codes, scales))

        for half, (codes, scales) in enumerate(quantised):
            for part in range(2):
                rows = slice(part * P, (part + 1) * P)
                bank = ps.tile([P, HALF], F32, name="y_%d_%d" % (half, part))
                nc.tensor.matmul_mx(
                    out=bank[:],
                    lhsT=v_picked[:, rows].bitcast(FP4X4),
                    lhsT_scale=v_picked_scales[:, rows],
                    rhs=codes[:].bitcast(FP8X4),
                    rhs_scale=scales[:],
                    start=True,
                    stop=True,
                )
                result = sb.tile([P, HALF], F32, name="result_%d_%d" % (half, part))
                dest = out[rows, half * HALF : (half + 1) * HALF]
                if part == 0:
                    nc.vector.tensor_copy(result[:], bank[:])
                    nc.sync.dma_start(dest, result[:])
                else:
                    nc.scalar.copy(result[:], bank[:])
                    nc.scalar.dma_start(dest, result[:])
